import numpy as np
import ml_dtypes


def mxq(x, axis, fmt="e4m3"):
    dtype, down = {"e4m3": (ml_dtypes.float8_e4m3fn, 7), "e5m2": (ml_dtypes.float8_e5m2, 14)}[fmt]
    v = np.moveaxis(np.asarray(x, np.float32).astype(ml_dtypes.bfloat16).astype(np.float64), axis, -1)
    blocks = v.reshape(v.shape[:-1] + (-1, 32))
    amax = np.abs(blocks).max(-1, keepdims=True)
    byte = np.maximum(np.where(amax > 0, np.frexp(amax)[1] - 1 + 127, 0) - down, 1)
    scale = np.exp2(byte - 127.0)
    codes = (blocks / scale).astype(np.float32).astype(dtype).astype(np.float64)
    return np.moveaxis((codes * scale).reshape(v.shape), -1, axis)


WIDE = False


def mx_kscale(k):
    if not WIDE:
        return np.ones(k)
    levels = np.array([30, -30])
    if k % 512:
        return np.exp2(np.random.permutation(np.resize(levels, k // 32))).repeat(32)
    a = np.empty((k // 512, 16))
    for p in range(k // 512):
        a[p, :8] = np.random.permutation(np.resize(levels, 8))
        for g in range(8):
            far = levels[np.abs(levels - a[p, g]) >= 10]
            a[p, g + 8] = far[np.random.randint(len(far))]
    return np.exp2(a.ravel()).repeat(32)


BF16 = ml_dtypes.bfloat16


def bf(x):
    return np.asarray(x, np.float32).astype(BF16)


def f64(x):
    return np.asarray(x).astype(np.float64)


V, K, A = 1024, 512, 2048


def setup_inputs():
    s = mx_kscale(K)
    rho = np.exp(0.3 * np.random.standard_normal((V, 1)))
    sr = rho * np.random.standard_normal((V, K))
    si = rho * 0.5 * np.random.standard_t(5, (V, K))
    energy = (sr * sr + si * si).sum(axis=1)
    ar = np.random.standard_normal((K, A))
    ai = np.random.standard_normal((K, A))
    norm = np.sqrt((ar * ar + ai * ai).sum(axis=0))
    return {"sig_re": bf(sr * s),
            "sig_im": bf(si * s),
            "dict_re": bf(ar / norm / s[:, None]),
            "dict_im": bf(ai / norm / s[:, None]),
            "inv_energy": bf(K / energy)}


def reference(sig_re, sig_im, dict_re, dict_im, inv_energy):
    cr = mxq(f64(sig_re), 1, "e4m3")
    ci = mxq(f64(sig_im), 1, "e5m2")
    dr = mxq(f64(dict_re), 0, "e4m3")
    di = mxq(f64(dict_im), 0, "e4m3")
    re = (cr @ dr) + (ci @ di)
    im = (ci @ dr) - (cr @ di)
    return (re * re + im * im) * f64(inv_energy)[:, None]

@@ -1,0 +1,212 @@
+from contextlib import ExitStack
+
+import concourse.mybir as mybir
+from concourse.masks import make_identity
+
+V, K, A = 1024, 512, 2048
+FLOPS = 4 * 2 * V * K * A
+
+F32 = mybir.dt.float32
+BF16 = mybir.dt.bfloat16
+U32 = mybir.dt.uint32
+U8 = mybir.dt.uint8
+E4M3 = mybir.dt.float8_e4m3fn_x4
+E5M2 = mybir.dt.float8_e5m2_x4
+ACT = mybir.ActivationFunctionType
+ALU = mybir.AluOpType
+
+P = 128
+PACK = 4
+N_TILE = 512
+V_TILES = V // P
+A_TILES = A // N_TILE
+PAIR = 2
+GROUPS = V_TILES // PAIR
+HALF = N_TILE // 2
+BANKS = 8
+ALIGN = 256
+
+
+def tile_fingerprint_match_score_s2_kernel(tc, sig_re, sig_im, dict_re, dict_im, inv_energy, out):
+    nc = tc.nc
+    with ExitStack() as ctx:
+        keep = ctx.enter_context(tc.tile_pool(name="keep", bufs=1))
+        stage = ctx.enter_context(tc.tile_pool(name="stage", bufs=2))
+        squares = ctx.enter_context(tc.tile_pool(name="squares", bufs=4))
+        results = ctx.enter_context(tc.tile_pool(name="results", bufs=10))
+        psum = ctx.enter_context(tc.psum_pool(name="psum", bufs=1))
+        ctx.enter_context(tc.manual_schedule())
+
+        sig_rows = {"re": sig_re.rearrange("(p i) k -> p (i k)", i=V_TILES),
+                    "im": sig_im.rearrange("(p i) k -> p (i k)", i=V_TILES)}
+        dict_rows = {"re": dict_re.rearrange("(p j) a -> p j a", j=PACK),
+                     "im": dict_im.rearrange("(p j) a -> p j a", j=PACK)}
+        out_rows = out.rearrange("(p i) a -> p i a", i=V_TILES)
+
+        sig_raw, dict_raw, sig_lined, dict_lined, sig_mx, dict_mx = {}, {}, {}, {}, {}, {}
+        sums, squared = {}, {}
+        banks_taken = []
+
+        def next_bank():
+            b = len(banks_taken) % BANKS
+            banks_taken.append(b)
+            return psum.tile([P, N_TILE], F32, name="bank%d" % b, tag="bank%d" % b)
+
+        def load_sig(part, g):
+            t = keep.tile([P, PAIR * K], BF16, name="sig_raw_%s%d" % (part, g), align_bytes=ALIGN)
+            nc.sync.dma_start(out=t[:], in_=sig_rows[part][:, g * PAIR * K:(g + 1) * PAIR * K])
+            sig_raw[part, g] = t
+
+        def load_dict(part, a):
+            t = keep.tile([P, PACK, N_TILE], BF16, name="dict_raw_%s%d" % (part, a), align_bytes=ALIGN)
+            nc.sync.dma_start(out=t[:], in_=dict_rows[part][:, :, a * N_TILE:(a + 1) * N_TILE])
+            dict_raw[part, a] = t
+
+        def mx_tiles(name, width):
+            codes = keep.tile([P, width], U32, name=name + "_codes", align_bytes=ALIGN)
+            scales = keep.tile([P, width], U8, name=name + "_scales", align_bytes=ALIGN)
+            return codes, scales
+
+        def turn_sig(part, g):
+            words = sig_raw[part, g][:].bitcast(F32)
+            bank = next_bank()
+            for j in range(PAIR):
+                for u in range(2):
+                    col = (2 * j + u) * P
+                    nc.tensor.transpose(bank[:, col:col + P], words[:, j * 256 + u:(j + 1) * 256:2], ident[:])
+            lined = stage.tile([P, PAIR * K], BF16, name="sig_lined_" + part, align_bytes=ALIGN)
+            nc.scalar.copy(out=lined[:].bitcast(F32).rearrange("p (j r u) -> p j r u", j=PAIR, u=2),
+                           in_=bank[:].rearrange("p (j u r) -> p j r u", j=PAIR, u=2))
+            sig_lined[part, g] = lined
+
+        def negate_sig(g):
+            lined = stage.tile([P, PAIR * K], BF16, name="sig_lined_neg", align_bytes=ALIGN)
+            nc.vector.tensor_scalar(out=lined[:], in0=sig_lined["re", g][:], scalar1=-1.0, scalar2=None, op0=ALU.mult)
+            sig_lined["neg", g] = lined
+
+        def quantize_sig(part, g):
+            codes, scales = mx_tiles("sig_%s%d" % (part, g), PAIR * P)
+            fmt = E5M2 if part == "im" else E4M3
+            nc.vector.quantize_mx(out=codes[:].bitcast(fmt), scales=scales[:], in_=sig_lined[part, g][:])
+            sig_mx[part, g] = (codes, scales, fmt)
+
+        def prepare_sig(g):
+            negate_sig(g)
+            quantize_sig("re", g)
+            quantize_sig("im", g)
+            quantize_sig("neg", g)
+
+        def line_dict(part, a, h):
+            lined = stage.tile([P, HALF * PACK], BF16, name="dict_lined", bufs=3, align_bytes=ALIGN)
+            nc.vector.tensor_copy(
+                out=lined[:].rearrange("p (c i t) -> p c t i", i=4, t=PACK),
+                in_=dict_raw[part, a][:, :, h * HALF:(h + 1) * HALF].rearrange("p t (c i) -> p c t i", i=4))
+            dict_lined[part, a, h] = lined
+
+        def quantize_dict(part, a, h):
+            if h == 0:
+                dict_mx[part, a] = mx_tiles("dict_%s%d" % (part, a), N_TILE)
+            codes, scales = dict_mx[part, a]
+            cols = slice(h * HALF, (h + 1) * HALF)
+            nc.vector.quantize_mx(out=codes[:, cols].bitcast(E4M3), scales=scales[:, cols],
+                                  in_=dict_lined[part, a, h][:])
+
+        def multiply(n, result, sig_part, dict_part):
+            a, i = divmod(n, V_TILES)
+            first = dict_part == "re"
+            if first:
+                sums[n, result] = next_bank()
+            s_codes, s_scales, fmt = sig_mx[sig_part, i // PAIR]
+            d_codes, d_scales = dict_mx[dict_part, a]
+            cols = slice((i % PAIR) * P, (i % PAIR + 1) * P)
+            nc.tensor.matmul_mx(out=sums[n, result][:], lhsT=s_codes[:, cols].bitcast(fmt), lhsT_scale=s_scales[:, cols],
+                                rhs=d_codes[:].bitcast(E4M3), rhs_scale=d_scales[:], start=first, stop=not first)
+
+        def square(n, result):
+            if result == "re":
+                squared[n] = squares.tile([P, 2, N_TILE], F32, name="squared")
+            i = n % V_TILES
+            nc.scalar.activation(out=squared[n][:, 0 if result == "re" else 1, :], in_=sums[n, result][:],
+                                 func=ACT.Square, scale=root[:, i:i + 1])
+
+        def finish(n):
+            a, i = divmod(n, V_TILES)
+            score = results.tile([P, N_TILE], F32, name="score")
+            nc.vector.tensor_tensor(out=score[:], in0=squared[n][:, 0, :], in1=squared[n][:, 1, :], op=ALU.add)
+            nc.sync.dma_start(out=out_rows[:, i, a * N_TILE:(a + 1) * N_TILE], in_=score[:])
+
+        energy = keep.tile([P, V_TILES], BF16, name="energy")
+        nc.sync.dma_start(out=energy[:], in_=inv_energy.rearrange("(p i) -> p i", i=V_TILES))
+        load_dict("re", 0)
+        load_sig("re", 0)
+        load_sig("im", 0)
+        load_dict("im", 0)
+        for g in (1, 2):
+            load_sig("re", g)
+            load_sig("im", g)
+        load_dict("re", 1)
+        load_sig("re", 3)
+        load_sig("im", 3)
+        load_dict("im", 1)
+        for a in range(2, A_TILES):
+            load_dict("re", a)
+            load_dict("im", a)
+
+        ident = keep.tile([P, P], F32, name="ident")
+        make_identity(nc, ident[:])
+        root = keep.tile([P, V_TILES], F32, name="root")
+        nc.scalar.activation(out=root[:], in_=energy[:], func=ACT.Sqrt)
+
+        turn_sig("re", 0)
+        turn_sig("im", 0)
+        line_dict("re", 0, 0)
+        line_dict("re", 0, 1)
+        quantize_dict("re", 0, 0)
+        quantize_dict("re", 0, 1)
+        quantize_sig("re", 0)
+        negate_sig(0)
+        line_dict("im", 0, 0)
+        quantize_sig("im", 0)
+        line_dict("im", 0, 1)
+        quantize_dict("im", 0, 0)
+        quantize_sig("neg", 0)
+        quantize_dict("im", 0, 1)
+        for n in range(PAIR):
+            multiply(n, "re", "re", "re")
+        turn_sig("re", 1)
+        turn_sig("im", 1)
+        for n in range(PAIR):
+            multiply(n, "im", "im", "re")
+        for n in range(PAIR):
+            multiply(n, "re", "im", "im")
+            multiply(n, "im", "neg", "im")
+        prepare_sig(1)
+        for n in range(PAIR):
+            square(n, "re")
+            square(n, "im")
+
+        pieces = [("re", 0), ("re", 1), ("im", 0), ("im", 1)]
+        for n in range(PAIR, V_TILES * A_TILES):
+            a, i = divmod(n, V_TILES)
+            ahead = i // PAIR + 1
+            turning = a == 0 and i % PAIR == 0 and ahead < GROUPS
+            if turning:
+                turn_sig("re", ahead)
+                turn_sig("im", ahead)
+            multiply(n, "re", "re", "re")
+            multiply(n, "re", "im", "im")
+            multiply(n, "im", "im", "re")
+            multiply(n, "im", "neg", "im")
+            square(n, "re")
+            square(n, "im")
+            k = i - PAIR
+            if a + 1 < A_TILES and 0 <= k < len(pieces):
+                line_dict(pieces[k][0], a + 1, pieces[k][1])
+            if n == PAIR:
+                finish(0)
+            finish(n - 1)
+            if a + 1 < A_TILES and 0 <= k - 1 < len(pieces):
+                quantize_dict(pieces[k - 1][0], a + 1, pieces[k - 1][1])
+            if turning:
+                prepare_sig(ahead)
+        finish(V_TILES * A_TILES - 1)

@@ -32,8 +32,8 @@ def tile_fingerprint_match_score_s2_kernel(tc, sig_re, sig_im, dict_re, dict_im,
     with ExitStack() as ctx:
         keep = ctx.enter_context(tc.tile_pool(name="keep", bufs=1))
         stage = ctx.enter_context(tc.tile_pool(name="stage", bufs=2))
-        squares = ctx.enter_context(tc.tile_pool(name="squares", bufs=4))
-        results = ctx.enter_context(tc.tile_pool(name="results", bufs=10))
+        squares = ctx.enter_context(tc.tile_pool(name="squares", bufs=7))
+        results = ctx.enter_context(tc.tile_pool(name="results", bufs=5))
         psum = ctx.enter_context(tc.psum_pool(name="psum", bufs=1))
         ctx.enter_context(tc.manual_schedule())
 
@@ -67,7 +67,7 @@ def tile_fingerprint_match_score_s2_kernel(tc, sig_re, sig_im, dict_re, dict_im,
             scales = keep.tile([P, width], U8, name=name + "_scales", align_bytes=ALIGN)
             return codes, scales
 
-        def turn_sig(part, g):
+        def turn_sig(part, g, copy):
             words = sig_raw[part, g][:].bitcast(F32)
             bank = next_bank()
             for j in range(PAIR):
@@ -75,7 +75,7 @@ def tile_fingerprint_match_score_s2_kernel(tc, sig_re, sig_im, dict_re, dict_im,
                     col = (2 * j + u) * P
                     nc.tensor.transpose(bank[:, col:col + P], words[:, j * 256 + u:(j + 1) * 256:2], ident[:])
             lined = stage.tile([P, PAIR * K], BF16, name="sig_lined_" + part, align_bytes=ALIGN)
-            nc.scalar.copy(out=lined[:].bitcast(F32).rearrange("p (j r u) -> p j r u", j=PAIR, u=2),
+            copy(out=lined[:].bitcast(F32).rearrange("p (j r u) -> p j r u", j=PAIR, u=2),
                            in_=bank[:].rearrange("p (j u r) -> p j r u", j=PAIR, u=2))
             sig_lined[part, g] = lined
 
@@ -96,20 +96,18 @@ def tile_fingerprint_match_score_s2_kernel(tc, sig_re, sig_im, dict_re, dict_im,
             quantize_sig("im", g)
             quantize_sig("neg", g)
 
-        def line_dict(part, a, h):
-            lined = stage.tile([P, HALF * PACK], BF16, name="dict_lined", bufs=3, align_bytes=ALIGN)
-            nc.vector.tensor_copy(
-                out=lined[:].rearrange("p (c i t) -> p c t i", i=4, t=PACK),
-                in_=dict_raw[part, a][:, :, h * HALF:(h + 1) * HALF].rearrange("p t (c i) -> p c t i", i=4))
-            dict_lined[part, a, h] = lined
+        def line_dict(part, a, c0, c1, copy):
+            if (part, a) not in dict_lined:
+                dict_lined[part, a] = stage.tile([P, N_TILE * PACK], BF16, name="dict_lined", bufs=3, align_bytes=ALIGN)
+            copy(out=dict_lined[part, a][:, c0 * PACK:c1 * PACK].rearrange("p (c i t) -> p c t i", i=4, t=PACK),
+                 in_=dict_raw[part, a][:, :, c0:c1].rearrange("p t (c i) -> p c t i", i=4))
 
-        def quantize_dict(part, a, h):
-            if h == 0:
+        def quantize_dict(part, a, c0, c1):
+            if (part, a) not in dict_mx:
                 dict_mx[part, a] = mx_tiles("dict_%s%d" % (part, a), N_TILE)
             codes, scales = dict_mx[part, a]
-            cols = slice(h * HALF, (h + 1) * HALF)
-            nc.vector.quantize_mx(out=codes[:, cols].bitcast(E4M3), scales=scales[:, cols],
-                                  in_=dict_lined[part, a, h][:])
+            nc.vector.quantize_mx(out=codes[:, c0:c1].bitcast(E4M3), scales=scales[:, c0:c1],
+                                  in_=dict_lined[part, a][:, c0 * PACK:c1 * PACK])
 
         def multiply(n, result, sig_part, dict_part):
             a, i = divmod(n, V_TILES)
@@ -122,28 +120,32 @@ def tile_fingerprint_match_score_s2_kernel(tc, sig_re, sig_im, dict_re, dict_im,
             nc.tensor.matmul_mx(out=sums[n, result][:], lhsT=s_codes[:, cols].bitcast(fmt), lhsT_scale=s_scales[:, cols],
                                 rhs=d_codes[:].bitcast(E4M3), rhs_scale=d_scales[:], start=first, stop=not first)
 
-        def square(n, result):
-            if result == "re":
-                squared[n] = squares.tile([P, 2, N_TILE], F32, name="squared")
+        def square(n, result, cols=slice(0, N_TILE)):
+            pair, j = divmod(n, PAIR)
+            if pair not in squared:
+                squared[pair] = squares.tile([P, 2, PAIR, N_TILE], F32, name="squared")
             i = n % V_TILES
-            nc.scalar.activation(out=squared[n][:, 0 if result == "re" else 1, :], in_=sums[n, result][:],
+            nc.scalar.activation(out=squared[pair][:, 0 if result == "re" else 1, j, cols], in_=sums[n, result][:, cols],
                                  func=ACT.Square, scale=root[:, i:i + 1])
 
-        def finish(n):
-            a, i = divmod(n, V_TILES)
-            score = results.tile([P, N_TILE], F32, name="score")
-            nc.vector.tensor_tensor(out=score[:], in0=squared[n][:, 0, :], in1=squared[n][:, 1, :], op=ALU.add)
-            nc.sync.dma_start(out=out_rows[:, i, a * N_TILE:(a + 1) * N_TILE], in_=score[:])
+        def finish(pair, tiles=slice(0, PAIR), cols=slice(0, N_TILE)):
+            a, i = divmod(pair * PAIR, V_TILES)
+            score = results.tile([P, tiles.stop - tiles.start, cols.stop - cols.start], F32, name="score")
+            nc.vector.tensor_tensor(out=score[:], in0=squared[pair][:, 0, tiles, cols], in1=squared[pair][:, 1, tiles, cols],
+                                    op=ALU.add)
+            nc.sync.dma_start(out=out_rows[:, i + tiles.start:i + tiles.stop,
+                                           a * N_TILE + cols.start:a * N_TILE + cols.stop], in_=score[:])
 
         energy = keep.tile([P, V_TILES], BF16, name="energy")
         nc.sync.dma_start(out=energy[:], in_=inv_energy.rearrange("(p i) -> p i", i=V_TILES))
-        load_dict("re", 0)
         load_sig("re", 0)
         load_sig("im", 0)
+        load_dict("re", 0)
+        load_sig("re", 1)
+        load_sig("im", 1)
         load_dict("im", 0)
-        for g in (1, 2):
-            load_sig("re", g)
-            load_sig("im", g)
+        load_sig("re", 2)
+        load_sig("im", 2)
         load_dict("re", 1)
         load_sig("re", 3)
         load_sig("im", 3)
@@ -151,62 +153,78 @@ def tile_fingerprint_match_score_s2_kernel(tc, sig_re, sig_im, dict_re, dict_im,
         for a in range(2, A_TILES):
             load_dict("re", a)
             load_dict("im", a)
-
         ident = keep.tile([P, P], F32, name="ident")
         make_identity(nc, ident[:])
         root = keep.tile([P, V_TILES], F32, name="root")
         nc.scalar.activation(out=root[:], in_=energy[:], func=ACT.Sqrt)
+        S, W = nc.scalar.copy, nc.vector.tensor_copy
 
-        turn_sig("re", 0)
-        turn_sig("im", 0)
-        line_dict("re", 0, 0)
-        line_dict("re", 0, 1)
-        quantize_dict("re", 0, 0)
-        quantize_dict("re", 0, 1)
+        DSTART, ASTART = 2, 6
+        turn_sig("re", 0, S)
+        line_dict("re", 0, 0, 320, W)
+        line_dict("re", 0, 320, 512, S)
+        turn_sig("im", 0, S)
         quantize_sig("re", 0)
-        negate_sig(0)
-        line_dict("im", 0, 0)
+        quantize_dict("re", 0, 0, 512)
+        turn_sig("re", 1, S)
         quantize_sig("im", 0)
-        line_dict("im", 0, 1)
-        quantize_dict("im", 0, 0)
+        turn_sig("im", 1, S)
+        for n in range(PAIR):
+            multiply(n, "re", "re", "re")
+        for n in range(PAIR):
+            multiply(n, "im", "im", "re")
+        negate_sig(0)
+        line_dict("im", 0, 0, 384, W)
+        line_dict("im", 0, 384, 512, S)
         quantize_sig("neg", 0)
-        quantize_dict("im", 0, 1)
-        for n in range(PAIR):
-            multiply(n, "re", "re", "re")
-        turn_sig("re", 1)
-        turn_sig("im", 1)
-        for n in range(PAIR):
-            multiply(n, "im", "im", "re")
-        for n in range(PAIR):
-            multiply(n, "re", "im", "im")
-            multiply(n, "im", "neg", "im")
+        quantize_dict("im", 0, 0, 512)
         prepare_sig(1)
-        for n in range(PAIR):
-            square(n, "re")
-            square(n, "im")
+        multiply(0, "re", "im", "im")
+        multiply(0, "im", "neg", "im")
+        square(0, "re")
+        square(0, "im")
+        turn_sig("re", 2, W)
+        turn_sig("im", 2, W)
+        prepare_sig(2)
+        multiply(1, "re", "im", "im")
+        multiply(1, "im", "neg", "im")
+        square(1, "re")
+        square(1, "im")
 
-        pieces = [("re", 0), ("re", 1), ("im", 0), ("im", 1)]
-        for n in range(PAIR, V_TILES * A_TILES):
-            a, i = divmod(n, V_TILES)
-            ahead = i // PAIR + 1
-            turning = a == 0 and i % PAIR == 0 and ahead < GROUPS
-            if turning:
-                turn_sig("re", ahead)
-                turn_sig("im", ahead)
+        last = V_TILES * A_TILES - 1
+        def tile_passes(n):
             multiply(n, "re", "re", "re")
             multiply(n, "re", "im", "im")
             multiply(n, "im", "im", "re")
             multiply(n, "im", "neg", "im")
+        added = 0
+        for n in range(PAIR, last):
+            a, i = divmod(n, V_TILES)
+            tile_passes(n)
             square(n, "re")
             square(n, "im")
-            k = i - PAIR
-            if a + 1 < A_TILES and 0 <= k < len(pieces):
-                line_dict(pieces[k][0], a + 1, pieces[k][1])
             if n == PAIR:
-                finish(0)
-            finish(n - 1)
-            if a + 1 < A_TILES and 0 <= k - 1 < len(pieces):
-                quantize_dict(pieces[k - 1][0], a + 1, pieces[k - 1][1])
-            if turning:
-                prepare_sig(ahead)
-        finish(V_TILES * A_TILES - 1)
+                line_dict("re", 1, 0, N_TILE, W)
+                turn_sig("re", 3, W)
+                turn_sig("im", 3, W)
+                prepare_sig(3)
+                line_dict("im", 1, 0, N_TILE, W)
+                quantize_dict("re", 1, 0, N_TILE)
+                quantize_dict("im", 1, 0, N_TILE)
+            elif 0 < a < A_TILES - 1 and i == DSTART:
+                line_dict("re", a + 1, 0, N_TILE, W)
+                line_dict("im", a + 1, 0, N_TILE, W)
+                quantize_dict("re", a + 1, 0, N_TILE)
+                quantize_dict("im", a + 1, 0, N_TILE)
+            elif n >= ASTART and added < (n + 1) // PAIR:
+                finish(added)
+                added += 1
+        tile_passes(last)
+        while added < last // PAIR:
+            finish(added)
+            added += 1
+        finish(added, slice(0, 1))
+        square(last, "re")
+        for cols in (slice(0, HALF), slice(HALF, N_TILE)):
+            square(last, "im", cols)
+            finish(added, slice(1, 2), cols)

@@ -21,18 +21,23 @@ N_TILE = 512
 V_TILES = V // P
 A_TILES = A // N_TILE
 PAIR = 2
-GROUPS = V_TILES // PAIR
-HALF = N_TILE // 2
+PAIRS = V_TILES // PAIR
+ROW_WORDS = K // 2
+WALK = 4
 BANKS = 8
 ALIGN = 256
+
+FIRST_SPLIT = {"re": 320, "im": 288}
+SINGLE_TILES = 4
 
 
 def tile_fingerprint_match_score_s2_kernel(tc, sig_re, sig_im, dict_re, dict_im, inv_energy, out):
     nc = tc.nc
+    on_scalar, on_vector = nc.scalar.copy, nc.vector.tensor_copy
     with ExitStack() as ctx:
         keep = ctx.enter_context(tc.tile_pool(name="keep", bufs=1))
-        stage = ctx.enter_context(tc.tile_pool(name="stage", bufs=2))
-        squares = ctx.enter_context(tc.tile_pool(name="squares", bufs=7))
+        stage = ctx.enter_context(tc.tile_pool(name="stage", bufs=3))
+        squares = ctx.enter_context(tc.tile_pool(name="squares", bufs=2 * PAIRS))
         results = ctx.enter_context(tc.tile_pool(name="results", bufs=5))
         psum = ctx.enter_context(tc.psum_pool(name="psum", bufs=1))
         ctx.enter_context(tc.manual_schedule())
@@ -43,7 +48,8 @@ def tile_fingerprint_match_score_s2_kernel(tc, sig_re, sig_im, dict_re, dict_im,
                      "im": dict_im.rearrange("(p j) a -> p j a", j=PACK)}
         out_rows = out.rearrange("(p i) a -> p i a", i=V_TILES)
 
-        sig_raw, dict_raw, sig_lined, dict_lined, sig_mx, dict_mx = {}, {}, {}, {}, {}, {}
+        sig_raw, sig_sorted, sig_lined, sig_mx = {}, {}, {}, {}
+        dict_raw, dict_lined, dict_mx = {}, {}, {}
         sums, squared = {}, {}
         banks_taken = []
 
@@ -53,30 +59,39 @@ def tile_fingerprint_match_score_s2_kernel(tc, sig_re, sig_im, dict_re, dict_im,
             return psum.tile([P, N_TILE], F32, name="bank%d" % b, tag="bank%d" % b)
 
         def load_sig(part, g):
-            t = keep.tile([P, PAIR * K], BF16, name="sig_raw_%s%d" % (part, g), align_bytes=ALIGN)
-            nc.sync.dma_start(out=t[:], in_=sig_rows[part][:, g * PAIR * K:(g + 1) * PAIR * K])
-            sig_raw[part, g] = t
+            raw = keep.tile([P, PAIR * K], BF16, name="sig_raw_%s%d" % (part, g), align_bytes=ALIGN)
+            nc.sync.dma_start(out=raw[:], in_=sig_rows[part][:, g * PAIR * K:(g + 1) * PAIR * K])
+            sig_raw[part, g] = raw
 
         def load_dict(part, a):
-            t = keep.tile([P, PACK, N_TILE], BF16, name="dict_raw_%s%d" % (part, a), align_bytes=ALIGN)
-            nc.sync.dma_start(out=t[:], in_=dict_rows[part][:, :, a * N_TILE:(a + 1) * N_TILE])
-            dict_raw[part, a] = t
+            raw = keep.tile([P, PACK, N_TILE], BF16, name="dict_raw_%s%d" % (part, a), align_bytes=ALIGN)
+            nc.sync.dma_start(out=raw[:], in_=dict_rows[part][:, :, a * N_TILE:(a + 1) * N_TILE])
+            dict_raw[part, a] = raw
 
         def mx_tiles(name, width):
             codes = keep.tile([P, width], U32, name=name + "_codes", align_bytes=ALIGN)
             scales = keep.tile([P, width], U8, name=name + "_scales", align_bytes=ALIGN)
             return codes, scales
 
+        def sort_sig(part, g, copy):
+            words = stage.tile([P, PAIR * ROW_WORDS], F32, name="sig_sorted", bufs=4, align_bytes=ALIGN)
+            copy(out=words[:].rearrange("p (j u m) -> p j u m", j=PAIR, u=2),
+                 in_=sig_raw[part, g][:].bitcast(F32).rearrange("p (j m u) -> p j u m", j=PAIR, u=2))
+            sig_sorted[part, g] = words
+
         def turn_sig(part, g, copy):
-            words = sig_raw[part, g][:].bitcast(F32)
             bank = next_bank()
             for j in range(PAIR):
                 for u in range(2):
-                    col = (2 * j + u) * P
-                    nc.tensor.transpose(bank[:, col:col + P], words[:, j * 256 + u:(j + 1) * 256:2], ident[:])
+                    cols = slice((2 * j + u) * P, (2 * j + u + 1) * P)
+                    if (part, g) in sig_sorted:
+                        words = sig_sorted[part, g][:, cols]
+                    else:
+                        words = sig_raw[part, g][:].bitcast(F32)[:, j * ROW_WORDS + u:(j + 1) * ROW_WORDS:2]
+                    nc.tensor.transpose(bank[:, cols], words, ident[:])
             lined = stage.tile([P, PAIR * K], BF16, name="sig_lined_" + part, align_bytes=ALIGN)
             copy(out=lined[:].bitcast(F32).rearrange("p (j r u) -> p j r u", j=PAIR, u=2),
-                           in_=bank[:].rearrange("p (j u r) -> p j r u", j=PAIR, u=2))
+                 in_=bank[:].rearrange("p (j u r) -> p j r u", j=PAIR, u=2))
             sig_lined[part, g] = lined
 
         def negate_sig(g):
@@ -90,141 +105,160 @@ def tile_fingerprint_match_score_s2_kernel(tc, sig_re, sig_im, dict_re, dict_im,
             nc.vector.quantize_mx(out=codes[:].bitcast(fmt), scales=scales[:], in_=sig_lined[part, g][:])
             sig_mx[part, g] = (codes, scales, fmt)
 
-        def prepare_sig(g):
+        def quantize_pair(g):
             negate_sig(g)
-            quantize_sig("re", g)
-            quantize_sig("im", g)
-            quantize_sig("neg", g)
+            for part in ("re", "im", "neg"):
+                quantize_sig(part, g)
 
-        def line_dict(part, a, c0, c1, copy):
-            if (part, a) not in dict_lined:
-                dict_lined[part, a] = stage.tile([P, N_TILE * PACK], BF16, name="dict_lined", bufs=3, align_bytes=ALIGN)
-            copy(out=dict_lined[part, a][:, c0 * PACK:c1 * PACK].rearrange("p (c i t) -> p c t i", i=4, t=PACK),
-                 in_=dict_raw[part, a][:, :, c0:c1].rearrange("p t (c i) -> p c t i", i=4))
+        def line_dict(part, a, shares):
+            lined = stage.tile([P, N_TILE * PACK], BF16, name="dict_lined", align_bytes=ALIGN)
+            for copy, c0, c1 in shares:
+                copy(out=lined[:, c0 * PACK:c1 * PACK].rearrange("p (c w t) -> p c t w", w=WALK, t=PACK),
+                     in_=dict_raw[part, a][:, :, c0:c1].rearrange("p t (c w) -> p c t w", w=WALK))
+            dict_lined[part, a] = lined
 
-        def quantize_dict(part, a, c0, c1):
-            if (part, a) not in dict_mx:
-                dict_mx[part, a] = mx_tiles("dict_%s%d" % (part, a), N_TILE)
-            codes, scales = dict_mx[part, a]
-            nc.vector.quantize_mx(out=codes[:, c0:c1].bitcast(E4M3), scales=scales[:, c0:c1],
-                                  in_=dict_lined[part, a][:, c0 * PACK:c1 * PACK])
+        def line_first_dict(part):
+            split = FIRST_SPLIT[part]
+            line_dict(part, 0, ((on_vector, 0, split), (on_scalar, split, N_TILE)))
 
-        def multiply(n, result, sig_part, dict_part):
+        def quantize_dict(part, a):
+            codes, scales = mx_tiles("dict_%s%d" % (part, a), N_TILE)
+            nc.vector.quantize_mx(out=codes[:].bitcast(E4M3), scales=scales[:], in_=dict_lined[part, a][:])
+            dict_mx[part, a] = (codes, scales)
+
+        def prepare_dict(a):
+            for part in ("re", "im"):
+                line_dict(part, a, ((on_vector, 0, N_TILE),))
+            for part in ("re", "im"):
+                quantize_dict(part, a)
+
+        def multiply(n, result, dict_part):
             a, i = divmod(n, V_TILES)
-            first = dict_part == "re"
-            if first:
+            opens = dict_part == "re"
+            if opens:
                 sums[n, result] = next_bank()
+                sig_part = result
+            else:
+                sig_part = "im" if result == "re" else "neg"
             s_codes, s_scales, fmt = sig_mx[sig_part, i // PAIR]
             d_codes, d_scales = dict_mx[dict_part, a]
             cols = slice((i % PAIR) * P, (i % PAIR + 1) * P)
             nc.tensor.matmul_mx(out=sums[n, result][:], lhsT=s_codes[:, cols].bitcast(fmt), lhsT_scale=s_scales[:, cols],
-                                rhs=d_codes[:].bitcast(E4M3), rhs_scale=d_scales[:], start=first, stop=not first)
+                                rhs=d_codes[:].bitcast(E4M3), rhs_scale=d_scales[:], start=opens, stop=not opens)
 
-        def square(n, result, cols=slice(0, N_TILE)):
+        def multiply_tile(n):
+            for result in ("re", "im"):
+                for dict_part in ("re", "im"):
+                    multiply(n, result, dict_part)
+
+        def square_slot(n, result):
             pair, j = divmod(n, PAIR)
             if pair not in squared:
                 squared[pair] = squares.tile([P, 2, PAIR, N_TILE], F32, name="squared")
+            return squared[pair][:, ("re", "im").index(result), j, :]
+
+        def square(n, result, cols=slice(0, N_TILE)):
             i = n % V_TILES
-            nc.scalar.activation(out=squared[pair][:, 0 if result == "re" else 1, j, cols], in_=sums[n, result][:, cols],
+            nc.scalar.activation(out=square_slot(n, result)[:, cols], in_=sums[n, result][:, cols],
                                  func=ACT.Square, scale=root[:, i:i + 1])
 
-        def finish(pair, tiles=slice(0, PAIR), cols=slice(0, N_TILE)):
+        def add_and_store(pair, tiles=slice(0, PAIR), cols=slice(0, N_TILE)):
             a, i = divmod(pair * PAIR, V_TILES)
             score = results.tile([P, tiles.stop - tiles.start, cols.stop - cols.start], F32, name="score")
-            nc.vector.tensor_tensor(out=score[:], in0=squared[pair][:, 0, tiles, cols], in1=squared[pair][:, 1, tiles, cols],
-                                    op=ALU.add)
+            nc.vector.tensor_tensor(out=score[:], in0=squared[pair][:, 0, tiles, cols],
+                                    in1=squared[pair][:, 1, tiles, cols], op=ALU.add)
             nc.sync.dma_start(out=out_rows[:, i + tiles.start:i + tiles.stop,
                                            a * N_TILE + cols.start:a * N_TILE + cols.stop], in_=score[:])
 
         energy = keep.tile([P, V_TILES], BF16, name="energy")
-        nc.sync.dma_start(out=energy[:], in_=inv_energy.rearrange("(p i) -> p i", i=V_TILES))
         load_sig("re", 0)
+        nc.sync.dma_start(out=energy[:], in_=inv_energy.rearrange("(p i) -> p i", i=V_TILES))
         load_sig("im", 0)
         load_dict("re", 0)
         load_sig("re", 1)
         load_sig("im", 1)
         load_dict("im", 0)
-        load_sig("re", 2)
-        load_sig("im", 2)
-        load_dict("re", 1)
-        load_sig("re", 3)
-        load_sig("im", 3)
-        load_dict("im", 1)
-        for a in range(2, A_TILES):
+        for g in range(2, PAIRS):
+            load_sig("re", g)
+            load_sig("im", g)
+        for a in range(1, A_TILES):
             load_dict("re", a)
             load_dict("im", a)
+
         ident = keep.tile([P, P], F32, name="ident")
         make_identity(nc, ident[:])
         root = keep.tile([P, V_TILES], F32, name="root")
         nc.scalar.activation(out=root[:], in_=energy[:], func=ACT.Sqrt)
-        S, W = nc.scalar.copy, nc.vector.tensor_copy
 
-        DSTART, ASTART = 2, 6
-        turn_sig("re", 0, S)
-        line_dict("re", 0, 0, 320, W)
-        line_dict("re", 0, 320, 512, S)
-        turn_sig("im", 0, S)
+        turn_sig("re", 0, on_scalar)
+        line_first_dict("re")
+        turn_sig("im", 0, on_scalar)
         quantize_sig("re", 0)
-        quantize_dict("re", 0, 0, 512)
-        turn_sig("re", 1, S)
+        quantize_dict("re", 0)
+        turn_sig("re", 1, on_scalar)
         quantize_sig("im", 0)
-        turn_sig("im", 1, S)
-        for n in range(PAIR):
-            multiply(n, "re", "re", "re")
-        for n in range(PAIR):
-            multiply(n, "im", "im", "re")
         negate_sig(0)
-        line_dict("im", 0, 0, 384, W)
-        line_dict("im", 0, 384, 512, S)
-        quantize_sig("neg", 0)
-        quantize_dict("im", 0, 0, 512)
-        prepare_sig(1)
-        multiply(0, "re", "im", "im")
-        multiply(0, "im", "neg", "im")
-        square(0, "re")
-        square(0, "im")
-        turn_sig("re", 2, W)
-        turn_sig("im", 2, W)
-        prepare_sig(2)
-        multiply(1, "re", "im", "im")
-        multiply(1, "im", "neg", "im")
-        square(1, "re")
-        square(1, "im")
+        line_first_dict("im")
+        turn_sig("im", 1, on_scalar)
 
-        last = V_TILES * A_TILES - 1
-        def tile_passes(n):
-            multiply(n, "re", "re", "re")
-            multiply(n, "re", "im", "im")
-            multiply(n, "im", "im", "re")
-            multiply(n, "im", "neg", "im")
+        for result in ("re", "im"):
+            for n in range(PAIR):
+                multiply(n, result, "re")
+        quantize_sig("neg", 0)
+        quantize_dict("im", 0)
+
+        sort_sig("re", 2, on_scalar)
+        sort_sig("im", 2, on_vector)
+        sort_sig("re", 3, on_vector)
+        sort_sig("im", 3, on_vector)
+        quantize_pair(1)
+        for n in range(PAIR):
+            for result in ("re", "im"):
+                multiply(n, result, "im")
+        for n in range(PAIR):
+            for result in ("re", "im"):
+                square(n, result)
+
+        for g, copy in ((2, on_vector), (3, on_scalar)):
+            turn_sig("re", g, copy)
+            turn_sig("im", g, copy)
+        quantize_pair(2)
+        quantize_pair(3)
+
         added = 0
-        for n in range(PAIR, last):
+        for n in range(PAIR, V_TILES * (A_TILES - 1)):
             a, i = divmod(n, V_TILES)
-            tile_passes(n)
+            multiply_tile(n)
             square(n, "re")
             square(n, "im")
-            if n == PAIR:
-                line_dict("re", 1, 0, N_TILE, W)
-                turn_sig("re", 3, W)
-                turn_sig("im", 3, W)
-                prepare_sig(3)
-                line_dict("im", 1, 0, N_TILE, W)
-                quantize_dict("re", 1, 0, N_TILE)
-                quantize_dict("im", 1, 0, N_TILE)
-            elif 0 < a < A_TILES - 1 and i == DSTART:
-                line_dict("re", a + 1, 0, N_TILE, W)
-                line_dict("im", a + 1, 0, N_TILE, W)
-                quantize_dict("re", a + 1, 0, N_TILE)
-                quantize_dict("im", a + 1, 0, N_TILE)
-            elif n >= ASTART and added < (n + 1) // PAIR:
-                finish(added)
-                added += 1
-        tile_passes(last)
-        while added < last // PAIR:
-            finish(added)
-            added += 1
-        finish(added, slice(0, 1))
+            if i == V_TILES // 2 - 1:
+                prepare_dict(a + 1)
+                while added < (n + 1) // PAIR:
+                    add_and_store(added)
+                    added += 1
+
+        n = V_TILES * (A_TILES - 1)
+        multiply_tile(n)
+        scaled = stage.tile([P, N_TILE], F32, name="scaled")
+        nc.vector.tensor_scalar(out=scaled[:], in0=sums[n, "re"][:], scalar1=energy[:, 0:1], scalar2=None, op0=ALU.mult)
+        add_and_store(added)
+        nc.vector.tensor_tensor(out=square_slot(n, "re"), in0=scaled[:], in1=sums[n, "re"][:], op=ALU.mult)
+        square(n, "im")
+        add_and_store(added + 1)
+
+        last = V_TILES * A_TILES - 1
+        for n in range(V_TILES * (A_TILES - 1) + 1, last):
+            pair, j = divmod(n, PAIR)
+            multiply_tile(n)
+            square(n, "re")
+            square(n, "im")
+            if n > last - SINGLE_TILES:
+                add_and_store(pair, slice(j, j + 1))
+            elif j == PAIR - 1:
+                add_and_store(pair)
+
+        multiply_tile(last)
         square(last, "re")
-        for cols in (slice(0, HALF), slice(HALF, N_TILE)):
+        for cols in (slice(0, N_TILE // 2), slice(N_TILE // 2, N_TILE)):
             square(last, "im", cols)
-            finish(added, slice(1, 2), cols)
+            add_and_store(last // PAIR, slice(PAIR - 1, PAIR), cols)

from contextlib import ExitStack

import concourse.mybir as mybir
from concourse.masks import make_identity

V, K, A = 1024, 512, 2048
FLOPS = 4 * 2 * V * K * A

F32 = mybir.dt.float32
BF16 = mybir.dt.bfloat16
U32 = mybir.dt.uint32
U8 = mybir.dt.uint8
E4M3 = mybir.dt.float8_e4m3fn_x4
E5M2 = mybir.dt.float8_e5m2_x4
ACT = mybir.ActivationFunctionType
ALU = mybir.AluOpType

P = 128
PACK = 4
N_TILE = 512
V_TILES = V // P
A_TILES = A // N_TILE
PAIR = 2
PAIRS = V_TILES // PAIR
ROW_WORDS = K // 2
WALK = 4
BANKS = 8
ALIGN = 256

FIRST_SPLIT = {"re": 320, "im": 288}
SINGLE_TILES = 4


def tile_fingerprint_match_score_s2_kernel(tc, sig_re, sig_im, dict_re, dict_im, inv_energy, out):
    nc = tc.nc
    on_scalar, on_vector = nc.scalar.copy, nc.vector.tensor_copy
    with ExitStack() as ctx:
        keep = ctx.enter_context(tc.tile_pool(name="keep", bufs=1))
        stage = ctx.enter_context(tc.tile_pool(name="stage", bufs=3))
        squares = ctx.enter_context(tc.tile_pool(name="squares", bufs=2 * PAIRS))
        results = ctx.enter_context(tc.tile_pool(name="results", bufs=5))
        psum = ctx.enter_context(tc.psum_pool(name="psum", bufs=1))
        ctx.enter_context(tc.manual_schedule())

        sig_rows = {"re": sig_re.rearrange("(p i) k -> p (i k)", i=V_TILES),
                    "im": sig_im.rearrange("(p i) k -> p (i k)", i=V_TILES)}
        dict_rows = {"re": dict_re.rearrange("(p j) a -> p j a", j=PACK),
                     "im": dict_im.rearrange("(p j) a -> p j a", j=PACK)}
        out_rows = out.rearrange("(p i) a -> p i a", i=V_TILES)

        sig_raw, sig_sorted, sig_lined, sig_mx = {}, {}, {}, {}
        dict_raw, dict_lined, dict_mx = {}, {}, {}
        sums, squared = {}, {}
        banks_taken = []

        def next_bank():
            b = len(banks_taken) % BANKS
            banks_taken.append(b)
            return psum.tile([P, N_TILE], F32, name="bank%d" % b, tag="bank%d" % b)

        def load_sig(part, g):
            raw = keep.tile([P, PAIR * K], BF16, name="sig_raw_%s%d" % (part, g), align_bytes=ALIGN)
            nc.sync.dma_start(out=raw[:], in_=sig_rows[part][:, g * PAIR * K:(g + 1) * PAIR * K])
            sig_raw[part, g] = raw

        def load_dict(part, a):
            raw = keep.tile([P, PACK, N_TILE], BF16, name="dict_raw_%s%d" % (part, a), align_bytes=ALIGN)
            nc.sync.dma_start(out=raw[:], in_=dict_rows[part][:, :, a * N_TILE:(a + 1) * N_TILE])
            dict_raw[part, a] = raw

        def mx_tiles(name, width):
            codes = keep.tile([P, width], U32, name=name + "_codes", align_bytes=ALIGN)
            scales = keep.tile([P, width], U8, name=name + "_scales", align_bytes=ALIGN)
            return codes, scales

        def sort_sig(part, g, copy):
            words = stage.tile([P, PAIR * ROW_WORDS], F32, name="sig_sorted", bufs=4, align_bytes=ALIGN)
            copy(out=words[:].rearrange("p (j u m) -> p j u m", j=PAIR, u=2),
                 in_=sig_raw[part, g][:].bitcast(F32).rearrange("p (j m u) -> p j u m", j=PAIR, u=2))
            sig_sorted[part, g] = words

        def turn_sig(part, g, copy):
            bank = next_bank()
            for j in range(PAIR):
                for u in range(2):
                    cols = slice((2 * j + u) * P, (2 * j + u + 1) * P)
                    if (part, g) in sig_sorted:
                        words = sig_sorted[part, g][:, cols]
                    else:
                        words = sig_raw[part, g][:].bitcast(F32)[:, j * ROW_WORDS + u:(j + 1) * ROW_WORDS:2]
                    nc.tensor.transpose(bank[:, cols], words, ident[:])
            lined = stage.tile([P, PAIR * K], BF16, name="sig_lined_" + part, align_bytes=ALIGN)
            copy(out=lined[:].bitcast(F32).rearrange("p (j r u) -> p j r u", j=PAIR, u=2),
                 in_=bank[:].rearrange("p (j u r) -> p j r u", j=PAIR, u=2))
            sig_lined[part, g] = lined

        def negate_sig(g):
            lined = stage.tile([P, PAIR * K], BF16, name="sig_lined_neg", align_bytes=ALIGN)
            nc.vector.tensor_scalar(out=lined[:], in0=sig_lined["re", g][:], scalar1=-1.0, scalar2=None, op0=ALU.mult)
            sig_lined["neg", g] = lined

        def quantize_sig(part, g):
            codes, scales = mx_tiles("sig_%s%d" % (part, g), PAIR * P)
            fmt = E5M2 if part == "im" else E4M3
            nc.vector.quantize_mx(out=codes[:].bitcast(fmt), scales=scales[:], in_=sig_lined[part, g][:])
            sig_mx[part, g] = (codes, scales, fmt)

        def quantize_pair(g):
            negate_sig(g)
            for part in ("re", "im", "neg"):
                quantize_sig(part, g)

        def line_dict(part, a, shares):
            lined = stage.tile([P, N_TILE * PACK], BF16, name="dict_lined", align_bytes=ALIGN)
            for copy, c0, c1 in shares:
                copy(out=lined[:, c0 * PACK:c1 * PACK].rearrange("p (c w t) -> p c t w", w=WALK, t=PACK),
                     in_=dict_raw[part, a][:, :, c0:c1].rearrange("p t (c w) -> p c t w", w=WALK))
            dict_lined[part, a] = lined

        def line_first_dict(part):
            split = FIRST_SPLIT[part]
            line_dict(part, 0, ((on_vector, 0, split), (on_scalar, split, N_TILE)))

        def quantize_dict(part, a):
            codes, scales = mx_tiles("dict_%s%d" % (part, a), N_TILE)
            nc.vector.quantize_mx(out=codes[:].bitcast(E4M3), scales=scales[:], in_=dict_lined[part, a][:])
            dict_mx[part, a] = (codes, scales)

        def prepare_dict(a):
            for part in ("re", "im"):
                line_dict(part, a, ((on_vector, 0, N_TILE),))
            for part in ("re", "im"):
                quantize_dict(part, a)

        def multiply(n, result, dict_part):
            a, i = divmod(n, V_TILES)
            opens = dict_part == "re"
            if opens:
                sums[n, result] = next_bank()
                sig_part = result
            else:
                sig_part = "im" if result == "re" else "neg"
            s_codes, s_scales, fmt = sig_mx[sig_part, i // PAIR]
            d_codes, d_scales = dict_mx[dict_part, a]
            cols = slice((i % PAIR) * P, (i % PAIR + 1) * P)
            nc.tensor.matmul_mx(out=sums[n, result][:], lhsT=s_codes[:, cols].bitcast(fmt), lhsT_scale=s_scales[:, cols],
                                rhs=d_codes[:].bitcast(E4M3), rhs_scale=d_scales[:], start=opens, stop=not opens)

        def multiply_tile(n):
            for result in ("re", "im"):
                for dict_part in ("re", "im"):
                    multiply(n, result, dict_part)

        def square_slot(n, result):
            pair, j = divmod(n, PAIR)
            if pair not in squared:
                squared[pair] = squares.tile([P, 2, PAIR, N_TILE], F32, name="squared")
            return squared[pair][:, ("re", "im").index(result), j, :]

        def square(n, result, cols=slice(0, N_TILE)):
            i = n % V_TILES
            nc.scalar.activation(out=square_slot(n, result)[:, cols], in_=sums[n, result][:, cols],
                                 func=ACT.Square, scale=root[:, i:i + 1])

        def add_and_store(pair, tiles=slice(0, PAIR), cols=slice(0, N_TILE)):
            a, i = divmod(pair * PAIR, V_TILES)
            score = results.tile([P, tiles.stop - tiles.start, cols.stop - cols.start], F32, name="score")
            nc.vector.tensor_tensor(out=score[:], in0=squared[pair][:, 0, tiles, cols],
                                    in1=squared[pair][:, 1, tiles, cols], op=ALU.add)
            nc.sync.dma_start(out=out_rows[:, i + tiles.start:i + tiles.stop,
                                           a * N_TILE + cols.start:a * N_TILE + cols.stop], in_=score[:])

        energy = keep.tile([P, V_TILES], BF16, name="energy")
        load_sig("re", 0)
        nc.sync.dma_start(out=energy[:], in_=inv_energy.rearrange("(p i) -> p i", i=V_TILES))
        load_sig("im", 0)
        load_dict("re", 0)
        load_sig("re", 1)
        load_sig("im", 1)
        load_dict("im", 0)
        for g in range(2, PAIRS):
            load_sig("re", g)
            load_sig("im", g)
        for a in range(1, A_TILES):
            load_dict("re", a)
            load_dict("im", a)

        ident = keep.tile([P, P], F32, name="ident")
        make_identity(nc, ident[:])
        root = keep.tile([P, V_TILES], F32, name="root")
        nc.scalar.activation(out=root[:], in_=energy[:], func=ACT.Sqrt)

        turn_sig("re", 0, on_scalar)
        line_first_dict("re")
        turn_sig("im", 0, on_scalar)
        quantize_sig("re", 0)
        quantize_dict("re", 0)
        turn_sig("re", 1, on_scalar)
        quantize_sig("im", 0)
        negate_sig(0)
        line_first_dict("im")
        turn_sig("im", 1, on_scalar)

        for result in ("re", "im"):
            for n in range(PAIR):
                multiply(n, result, "re")
        quantize_sig("neg", 0)
        quantize_dict("im", 0)

        sort_sig("re", 2, on_scalar)
        sort_sig("im", 2, on_vector)
        sort_sig("re", 3, on_vector)
        sort_sig("im", 3, on_vector)
        quantize_pair(1)
        for n in range(PAIR):
            for result in ("re", "im"):
                multiply(n, result, "im")
        for n in range(PAIR):
            for result in ("re", "im"):
                square(n, result)

        for g, copy in ((2, on_vector), (3, on_scalar)):
            turn_sig("re", g, copy)
            turn_sig("im", g, copy)
        quantize_pair(2)
        quantize_pair(3)

        added = 0
        for n in range(PAIR, V_TILES * (A_TILES - 1)):
            a, i = divmod(n, V_TILES)
            multiply_tile(n)
            square(n, "re")
            square(n, "im")
            if i == V_TILES // 2 - 1:
                prepare_dict(a + 1)
                while added < (n + 1) // PAIR:
                    add_and_store(added)
                    added += 1

        n = V_TILES * (A_TILES - 1)
        multiply_tile(n)
        scaled = stage.tile([P, N_TILE], F32, name="scaled")
        nc.vector.tensor_scalar(out=scaled[:], in0=sums[n, "re"][:], scalar1=energy[:, 0:1], scalar2=None, op0=ALU.mult)
        add_and_store(added)
        nc.vector.tensor_tensor(out=square_slot(n, "re"), in0=scaled[:], in1=sums[n, "re"][:], op=ALU.mult)
        square(n, "im")
        add_and_store(added + 1)

        last = V_TILES * A_TILES - 1
        for n in range(V_TILES * (A_TILES - 1) + 1, last):
            pair, j = divmod(n, PAIR)
            multiply_tile(n)
            square(n, "re")
            square(n, "im")
            if n > last - SINGLE_TILES:
                add_and_store(pair, slice(j, j + 1))
            elif j == PAIR - 1:
                add_and_store(pair)

        multiply_tile(last)
        square(last, "re")
        for cols in (slice(0, N_TILE // 2), slice(N_TILE // 2, N_TILE)):
            square(last, "im", cols)
            add_and_store(last // PAIR, slice(PAIR - 1, PAIR), cols)
